import numpy as np
import ml_dtypes


def mxq(x, axis, fmt="e4m3"):
    dtype, down = {"e4m3": (ml_dtypes.float8_e4m3fn, 7), "e5m2": (ml_dtypes.float8_e5m2, 14)}[fmt]
    v = np.moveaxis(np.asarray(x, np.float32).astype(ml_dtypes.bfloat16).astype(np.float64), axis, -1)
    blocks = v.reshape(v.shape[:-1] + (-1, 32))
    amax = np.abs(blocks).max(-1, keepdims=True)
    byte = np.maximum(np.where(amax > 0, np.frexp(amax)[1] - 1 + 127, 0) - down, 1)
    scale = np.exp2(byte - 127.0)
    codes = (blocks / scale).astype(np.float32).astype(dtype).astype(np.float64)
    return np.moveaxis((codes * scale).reshape(v.shape), -1, axis)


WIDE = False


def mx_kscale(k):
    if not WIDE:
        return np.ones(k)
    levels = np.array([10, -10, 5, -5, 0])
    if k % 512:
        return np.exp2(np.random.permutation(np.resize(levels, k // 32))).repeat(32)
    a = np.empty((k // 512, 16))
    for p in range(k // 512):
        a[p, :8] = np.random.permutation(np.resize(levels, 8))
        for g in range(8):
            far = levels[np.abs(levels - a[p, g]) >= 10]
            a[p, g + 8] = far[np.random.randint(len(far))]
    return np.exp2(a.ravel()).repeat(32)


BF16 = ml_dtypes.bfloat16


def bf(x):
    return np.asarray(x, np.float32).astype(BF16)


def f64(x):
    return np.asarray(x).astype(np.float64)


E2M1 = np.array([0.0, 0.5, 1.0, 1.5, 2.0, 3.0, 4.0, 6.0, -0.0, -0.5, -1.0, -1.5, -2.0, -3.0, -4.0, -6.0])


def pack_weight(w, fmt):
    k, n = w.shape
    w = f64(bf(w)).reshape(k // 32, 32, n)
    amax = np.abs(w).max(1)
    if fmt == "e4m3":
        byte = np.frexp(amax)[1] - 1 + 127 - 7
    else:
        mant, ex = np.frexp(amax / 6.0)
        byte = np.where(mant > 0.5, ex, ex - 1) + 127
    byte = np.clip(np.where(amax > 0, byte, 1), 1, 254)
    scaled = (w * np.exp2(127.0 - byte)[:, None, :]).reshape(k, n).astype(np.float32)
    by_word = np.ascontiguousarray(scaled.reshape(k // 512, 128, 4, n).transpose(0, 1, 3, 2))
    if fmt == "e4m3":
        words = by_word.astype(ml_dtypes.float8_e4m3fn).view(np.uint8)
    else:
        c = by_word.astype(ml_dtypes.float4_e2m1fn).view(np.uint8) & 0xF
        words = c[..., 0::2] | (c[..., 1::2] << 4)
    return np.ascontiguousarray(words), np.ascontiguousarray(byte.astype(np.uint8).reshape(k // 512, 16, n))


def unpack_weight(words, scales, fmt):
    g, p, n, _ = words.shape
    if fmt == "e4m3":
        vals = np.ascontiguousarray(words).view(ml_dtypes.float8_e4m3fn).astype(np.float64)
    else:
        nib = np.empty((g, p, n, 4), np.uint8)
        nib[..., 0::2] = words & 0xF
        nib[..., 1::2] = words >> 4
        vals = E2M1[nib]
    vals = vals * np.repeat(np.exp2(scales.astype(np.float64) - 127.0), 8, axis=1)[..., None]
    return vals.transpose(0, 1, 3, 2).reshape(g * 512, n)
def pack4(w):
    words, scales = pack_weight(w, "e2m1")
    return words.reshape(words.shape[0], 128, -1), scales


def unpack4(words, scales):
    return unpack_weight(words.reshape(words.shape[0], 128, -1, 2), scales, "e2m1")


M, A, B, U = 1536, 1024, 512, 256


def setup_inputs():
    s, t = mx_kscale(2 * A), mx_kscale(2 * B)
    x = np.random.standard_normal((2 * A, M)) * s[:, None]
    place = np.random.uniform(-1.0, 1.0, A) * np.pi * A / 2
    direction = np.random.uniform(-1.0, 1.0, B)
    phase = place[:, None] * direction[None, :]
    co, si = np.cos(phase) / np.sqrt(A), np.sin(phase) / np.sqrt(A)
    steer = np.concatenate([np.concatenate([co, -si], axis=1), np.concatenate([si, co], axis=1)], axis=0) / s[:, None]
    vr = np.random.standard_normal((B, U)) / np.sqrt(B)
    vi = np.random.standard_normal((B, U)) / np.sqrt(B)
    comb = np.concatenate([np.concatenate([vr, vi], axis=1), np.concatenate([-vi, vr], axis=1)], axis=0) / t[:, None]
    x_words, x_scales = pack4(x)
    s_words, s_scales = pack4(steer)
    c_words, c_scales = pack4(comb)
    return {"x_words": x_words, "x_scales": x_scales,
            "s_words": s_words, "s_scales": s_scales,
            "phi": bf(np.random.uniform(-1.5, 1.5, B)),
            "noise": bf(np.random.uniform(0.5, 1.5, B)),
            "gain": bf((1 + 0.1 * np.random.standard_normal(2 * B)) * t),
            "c_words": c_words, "c_scales": c_scales}


def reference(x_words, x_scales, s_words, s_scales, phi, noise, gain, c_words, c_scales):
    y = unpack4(x_words, x_scales).T @ unpack4(s_words, s_scales)
    yr, yi = y[:, :B], y[:, B:]
    power = yr * yr + yi * yi
    f = power / (power + f64(noise)[None, :])
    c, d = np.cos(f64(phi))[None, :], np.sin(f64(phi))[None, :]
    zr = f * (c * yr - d * yi)
    zi = f * (d * yr + c * yi)
    z = np.concatenate([zr, zi], axis=1) * f64(gain)[None, :]
    return mxq(z, 1, "e4m3") @ unpack4(c_words, c_scales)

@@ -1,0 +1,322 @@
+from contextlib import ExitStack
+
+import concourse.mybir as mybir
+
+FLOPS = 2 * 1536 * 2048 * 1024 + 2 * 1536 * 1024 * 512
+
+F32 = mybir.dt.float32
+BF16 = mybir.dt.bfloat16
+I32 = mybir.dt.int32
+U32 = mybir.dt.uint32
+U8 = mybir.dt.uint8
+FP8X4 = mybir.dt.float8_e4m3fn_x4
+FP4X4 = mybir.dt.float4_e2m1fn_x4
+ACT = mybir.ActivationFunctionType
+MUL = mybir.AluOpType.mult
+ADD = mybir.AluOpType.add
+
+P = 128
+G = 4
+T = 4
+W = 256
+SB = 256
+WIDTHS = [256,256,256,256,256,256]
+STARTS = [sum(WIDTHS[:c]) for c in range(len(WIDTHS))]
+CHUNKS = len(WIDTHS)
+PAIRS = CHUNKS * T
+FILL = 2
+O_ON_S = [0]
+O_MOD = 2
+
+
+def tile_postfiltered_beam_combining_f2_kernel(
+    tc, x_words, x_scales, s_words, s_scales, phi, noise, gain, c_words, c_scales, out
+):
+    nc = tc.nc
+    with ExitStack() as ctx:
+        keep = ctx.enter_context(tc.tile_pool(name="keep", bufs=1))
+        work = ctx.enter_context(tc.tile_pool(name="work", bufs=3))
+        wide = ctx.enter_context(tc.tile_pool(name="wide", bufs=2))
+        psum = ctx.enter_context(tc.psum_pool(name="psum", bufs=6))
+        psum_o = ctx.enter_context(tc.psum_pool(name="psum_o", bufs=2))
+        ctx.enter_context(tc.manual_schedule())
+
+        W0 = WIDTHS[0]
+        WR = 1536 - W0
+        s_raw = [keep.tile([P, 2, 2048], U8, name="s_raw%d" % g, align_bytes=64) for g in range(2)]
+        s_sraw = keep.tile([P, G, 1024], U8, align_bytes=64)
+        s_cod = [keep.tile([P, G, 2, 256], U8, name="s_cod%d" % t, align_bytes=64) for t in range(T)]
+        s_sca = [keep.tile([P, G, 2, 128], U8, name="s_sca%d" % t, align_bytes=64) for t in range(T)]
+        x_cod = [keep.tile([P, G, 2 * w], U8, name="x_cod%d" % c, align_bytes=64) for c, w in enumerate(WIDTHS)]
+        x_sca0 = keep.tile([P, G, W0], U8, align_bytes=64)
+        x_scar = keep.tile([P, G, WR], U8, align_bytes=64)
+        c_cod = keep.tile([P, 2, 1024], U8, align_bytes=64)
+        c_sca = keep.tile([P, 2, 512], U8, align_bytes=64)
+        ph = keep.tile([P, T], BF16)
+        nz_b = keep.tile([P, T], BF16)
+        gn = keep.tile([P, 2, T], BF16)
+        nz = keep.tile([P, T], F32)
+        sd = keep.tile([P, T], F32)
+        sh = keep.tile([P, T], F32)
+        s2 = keep.tile([P, T], F32)
+        cc = keep.tile([P, T], F32)
+        nd = keep.tile([P, T], F32)
+        cgr = keep.tile([P, T], F32)
+        cgi = keep.tile([P, T], F32)
+        ndgr = keep.tile([P, T], F32)
+        dgi = keep.tile([P, T], F32)
+        dummy = keep.tile([P, T], F32)
+
+        def fill_zero(eng, plane):
+            eng.memset(plane[:].rearrange("p g n -> p (g n)").bitcast(I32), 0)
+
+        def x_scale(c):
+            if c == 0:
+                return x_sca0[:]
+            return x_scar[:, :, STARTS[c] - W0 : STARTS[c] - W0 + WIDTHS[c]]
+
+        fill_zero(nc.vector, s_sraw)
+        fill_zero(nc.gpsimd, x_sca0)
+
+        xs_view = x_scales.rearrange("g (q r) n -> q r g n", r=4)
+        ss_view = s_scales.rearrange("g (q r) n -> q r g n", r=4)
+        cs_view = c_scales.rearrange("g (q r) n -> q r g n", r=4)
+        xw_view = x_words.rearrange("g p b -> p g b")
+        sw_view = s_words.rearrange("g p b -> p g b")
+        cw_view = c_words.rearrange("g p b -> p g b")
+
+        def load_x(c):
+            a = 2 * STARTS[c]
+            nc.sync.dma_start(
+                out=x_cod[c][:].bitcast(I32), in_=xw_view[:, :, a : a + 2 * WIDTHS[c]].bitcast(I32)
+            )
+
+        def load_rows(eng, plane, view):
+            for q in range(4):
+                eng.dma_start(out=plane[32 * q : 32 * q + 4, :, :].bitcast(I32), in_=view[q].bitcast(I32))
+
+        nc.gpsimd.dma_start(out=ph[:], in_=phi.rearrange("(p t) -> p t", t=T))
+        nc.gpsimd.dma_start(out=nz_b[:], in_=noise.rearrange("(p t) -> p t", t=T))
+        nc.gpsimd.dma_start(out=gn[:], in_=gain.rearrange("(h p t) -> p h t", h=2, t=T))
+        fill_zero(nc.gpsimd, x_scar)
+        fill_zero(nc.gpsimd, c_sca)
+        for k in range(2):
+            nc.sync.dma_start(out=s_raw[k][:].bitcast(I32), in_=sw_view[:, 2 * k : 2 * k + 2, :].bitcast(I32))
+        load_rows(nc.scalar, s_sraw, ss_view)
+        load_x(0)
+        load_rows(nc.sync, x_sca0, xs_view[:, :, :, 0:W0])
+        load_x(1)
+        load_rows(nc.sync, x_scar, xs_view[:, :, :, W0:1536])
+        for c in range(2, CHUNKS):
+            load_x(c)
+        load_rows(nc.sync, c_sca, cs_view)
+        nc.sync.dma_start(out=c_cod[:].bitcast(I32), in_=cw_view.bitcast(I32))
+
+        nc.scalar.activation(out=sd[:], in_=ph[:], func=ACT.Sin)
+        nc.scalar.activation(out=sh[:], in_=ph[:], func=ACT.Sin, scale=0.5)
+        nc.gpsimd.tensor_copy(out=nz[:], in_=nz_b[:])
+        nc.scalar.activation(out=dummy[:], in_=nz[:], func=ACT.Abs_reciprocal_sqrt)
+        nc.gpsimd.tensor_tensor(out=s2[:], in0=sh[:], in1=sh[:], op=MUL)
+        nc.gpsimd.tensor_scalar(out=cc[:], in0=s2[:], scalar1=-2.0, scalar2=1.0, op0=MUL, op1=ADD)
+        nc.gpsimd.tensor_scalar(out=nd[:], in0=sd[:], scalar1=-1.0, scalar2=0.0, op0=MUL, op1=ADD)
+        nc.gpsimd.tensor_tensor(out=ndgr[:], in0=nd[:], in1=gn[:, 0, :], op=MUL)
+        nc.gpsimd.tensor_tensor(out=dgi[:], in0=sd[:], in1=gn[:, 1, :], op=MUL)
+        nc.gpsimd.tensor_tensor(out=cgr[:], in0=cc[:], in1=gn[:, 0, :], op=MUL)
+        nc.gpsimd.tensor_tensor(out=cgi[:], in0=cc[:], in1=gn[:, 1, :], op=MUL)
+
+        def permute_codes(t, k):
+            nc.vector.tensor_copy(
+                out=s_cod[t][:, 2 * k : 2 * k + 2, :, :].rearrange("p g h (m e) -> p (g h) m e", e=2),
+                in_=s_raw[k][:].rearrange("p g (h m t e) -> p (g h) m t e", h=2, t=T, e=2)[:, :, :, t, :],
+            )
+
+        def permute_scales(t):
+            nc.vector.tensor_copy(
+                out=s_sca[t][:].rearrange("p g h m -> p (g h) m"),
+                in_=s_sraw[:].rearrange("p g (h m t) -> p (g h) m t", h=2, t=T)[:, :, :, t],
+            )
+
+        y = [None] * PAIRS
+        sq = [None] * PAIRS
+        ab = [None] * PAIRS
+        pw = [None] * PAIRS
+        rs = [None] * PAIRS
+        r2 = [None] * PAIRS
+        uv = [None] * CHUNKS
+        ff = [None] * CHUNKS
+        zt = {}
+        zc = {}
+        zs = {}
+        oo = {}
+
+        def steer(j):
+            c, t = divmod(j, T)
+            y[j] = psum.tile([P, 2, W], F32, name="y")
+            for h in range(2):
+                for g in range(G):
+                    nc.tensor.matmul_mx(
+                        out=y[j][:, h, :],
+                        lhsT=s_cod[t][:, g, h, :].bitcast(FP4X4),
+                        lhsT_scale=s_sca[t][:, g, h, :],
+                        rhs=x_cod[c][:, g, :].bitcast(FP4X4),
+                        rhs_scale=x_scale(c)[:, g, :],
+                        start=(g == 0),
+                        stop=(g == G - 1),
+                    )
+
+        def square(j):
+            sq[j] = work.tile([P, 2, W], F32, name="sq")
+            nc.scalar.activation(out=sq[j][:], in_=y[j][:], func=ACT.Square)
+
+        def cross(j, h):
+            c, t = divmod(j, T)
+            if h == 0:
+                ab[j] = work.tile([P, 2, W], F32, name="ab")
+            k = (ndgr, dgi)[h]
+            nc.scalar.activation(out=ab[j][:, h, :], in_=y[j][:, 1 - h, :], func=ACT.Copy, scale=k[:, t : t + 1])
+
+        def power(j):
+            if j % 2 == 0:
+                pw[j // 2] = work.tile([P, 2, W], F32, name="pw")
+            nc.gpsimd.tensor_tensor(out=pw[j // 2][:, j % 2, :], in0=sq[j][:, 0, :], in1=sq[j][:, 1, :], op=ADD)
+
+        def rotate(j, h):
+            c, t = divmod(j, T)
+            if t == 0 and h == 0:
+                uv[c] = wide.tile([P, T, 2, W], F32, name="uv")
+            k = (cgr, cgi)[h]
+            nc.vector.scalar_tensor_tensor(
+                out=uv[c][:, t, h, :], in0=y[j][:, h, :], scalar=k[:, t : t + 1], in1=ab[j][:, h, :], op0=MUL, op1=ADD
+            )
+
+        def inverse_root(j):
+            t = j % T
+            if j % 2 == 0:
+                rs[j // 2] = work.tile([P, 2, W], F32, name="rs")
+            nc.scalar.activation(
+                out=rs[j // 2][:, j % 2, :], in_=pw[j // 2][:, j % 2, :], func=ACT.Abs_reciprocal_sqrt, bias=nz[:, t : t + 1]
+            )
+
+        def inverse(d):
+            r2[d] = work.tile([P, 2, W], F32, name="r2")
+            nc.scalar.activation(out=r2[d][:], in_=rs[d][:], func=ACT.Square)
+
+        def wiener(d):
+            c, e = divmod(d, T // 2)
+            if e == 0:
+                ff[c] = wide.tile([P, T, W], F32, name="ff")
+            nc.vector.tensor_tensor(out=ff[c][:, 2 * e : 2 * e + 2, :], in0=pw[d][:], in1=r2[d][:], op=MUL)
+
+        def weigh(c, b, h):
+            sb = min(SB, WIDTHS[c])
+            if h == 0:
+                zt[c, b] = wide.tile([P, 2, sb, T], BF16, name="zt", align_bytes=64)
+            cols = slice(b * sb, (b + 1) * sb)
+            nc.vector.tensor_tensor(
+                out=zt[c, b][:, h, :, :].rearrange("p (c i) t -> p c t i", i=4),
+                in0=uv[c][:, :, h, cols].rearrange("p t (c i) -> p c t i", i=4),
+                in1=ff[c][:, :, cols].rearrange("p t (c i) -> p c t i", i=4),
+                op=MUL,
+            )
+
+        def quantise(c, b):
+            sb = min(SB, WIDTHS[c])
+            zc[c, b] = wide.tile([P, 2, sb], U32, name="zc", align_bytes=64)
+            zs[c, b] = wide.tile([P, 2, sb], U8, name="zs", align_bytes=64)
+            nc.vector.quantize_mx(
+                out=zc[c, b][:].rearrange("p h n -> p (h n)").bitcast(FP8X4),
+                scales=zs[c, b][:].rearrange("p h n -> p (h n)"),
+                in_=zt[c, b][:].rearrange("p h n t -> p (h n t)"),
+            )
+
+        def combine(c, b, k):
+            o = psum_o.tile([P, 512], F32, name="o")
+            oo[c, b, k] = o
+            for h in range(2):
+                nc.tensor.matmul_mx(
+                    out=o[:],
+                    lhsT=zc[c, b][:, h, k * P : (k + 1) * P].bitcast(FP8X4),
+                    lhsT_scale=zs[c, b][:, h, k * P : (k + 1) * P],
+                    rhs=c_cod[:, h, :].bitcast(FP4X4),
+                    rhs_scale=c_sca[:, h, :],
+                    start=(h == 0),
+                    stop=(h == 1),
+                )
+
+        def store(c, b, k):
+            sb = min(SB, WIDTHS[c])
+            r0 = STARTS[c] + b * sb + k * P
+            res = work.tile([P, 512], F32, name="res")
+            if (r0 // P) % O_MOD in O_ON_S:
+                nc.scalar.copy(out=res[:], in_=oo[c, b, k][:])
+            else:
+                nc.vector.tensor_copy(out=res[:], in_=oo[c, b, k][:])
+            nc.sync.dma_start(out=out[r0 : r0 + P, :], in_=res[:])
+
+        v_queue = []
+        pe_queue = []
+        o_queue = []
+
+        def chunk_done(c):
+            sb = min(SB, WIDTHS[c])
+            nb = WIDTHS[c] // sb
+            for b in range(nb):
+                v_queue.append(("F", c, b, 0))
+                if b > 0:
+                    v_queue.append(("Q", c, b - 1, 0))
+                v_queue.append(("F", c, b, 1))
+            v_queue.append(("Q", c, nb - 1, 0))
+
+        def v_pop(n):
+            for i in range(min(n, len(v_queue))):
+                kind, c, b, h = v_queue.pop(0)
+                if kind == "F":
+                    weigh(c, b, h)
+                else:
+                    quantise(c, b)
+                    for k in range(min(SB, WIDTHS[c]) // P):
+                        pe_queue.append((c, b, k))
+
+        permute_codes(0, 0)
+        permute_scales(0)
+        permute_codes(0, 1)
+        permute_codes(1, 0)
+        permute_codes(1, 1)
+        permute_scales(1)
+        steer(0)
+        for j in range(PAIRS + 12):
+            if j + 2 < T:
+                permute_codes(j + 2, 0)
+                permute_codes(j + 2, 1)
+                permute_scales(j + 2)
+            for i in (2 * j + 1, 2 * j + 2) if j == 0 else (j + 2,):
+                if i < PAIRS:
+                    steer(i)
+            for i in range(min(2, len(pe_queue))):
+                key = pe_queue.pop(0)
+                combine(*key)
+                o_queue.append(key)
+            if j < PAIRS:
+                square(j)
+                power(j)
+            if 0 < j <= PAIRS:
+                inverse_root(j - 1)
+            if j < PAIRS:
+                cross(j, 0)
+            if 0 < j <= PAIRS and j % 2 == 0:
+                inverse(j // 2 - 1)
+            if j < PAIRS:
+                cross(j, 1)
+            if 0 < j <= PAIRS:
+                rotate(j - 1, 0)
+                rotate(j - 1, 1)
+            if 1 < j <= PAIRS + 1 and j % 2 == 1:
+                wiener(j // 2 - 1)
+                if (j - 2) % T == T - 1:
+                    chunk_done((j - 2) // T)
+            n = 1 if j < PAIRS else 2
+            while n > 0 and v_queue:
+                n -= v_queue[0][0] == "F"
+                v_pop(1)
+            while len(o_queue) > (0 if j > PAIRS else 2):
+                store(*o_queue.pop(0))

@@ -18,15 +18,26 @@ ADD = mybir.AluOpType.add
 P = 128
 G = 4
 T = 4
+M = 1536
 W = 256
-SB = 256
-WIDTHS = [256,256,256,256,256,256]
-STARTS = [sum(WIDTHS[:c]) for c in range(len(WIDTHS))]
-CHUNKS = len(WIDTHS)
+CHUNKS = M // W
 PAIRS = CHUNKS * T
-FILL = 2
-O_ON_S = [0]
-O_MOD = 2
+O_ON_S = [0, 2, 4, 6, 8, 10, 11]
+P_ON_V = []
+R2_ON_V = []
+R2_ON_G = []
+TAIL_FREE = 0
+PW_BUFS = 3
+AB_BUFS = 3
+P_LAG = 1
+ARS_LAG = 2
+ROT_LAG = 1
+WIEN_LAG = 3
+C_LAG = 1
+O_LAG = 1
+AHEAD = 2
+F_STEP = 1
+FI = 2
 
 
 def tile_postfiltered_beam_combining_f2_kernel(
@@ -36,20 +47,21 @@ def tile_postfiltered_beam_combining_f2_kernel(
     with ExitStack() as ctx:
         keep = ctx.enter_context(tc.tile_pool(name="keep", bufs=1))
         work = ctx.enter_context(tc.tile_pool(name="work", bufs=3))
-        wide = ctx.enter_context(tc.tile_pool(name="wide", bufs=2))
+        cross_pool = ctx.enter_context(tc.tile_pool(name="cross", bufs=AB_BUFS))
+        power_pool = ctx.enter_context(tc.tile_pool(name="power", bufs=PW_BUFS))
+        free_pool = ctx.enter_context(tc.tile_pool(name="free", bufs=4))
+        wide = ctx.enter_context(tc.tile_pool(name="wide", bufs=3))
         psum = ctx.enter_context(tc.psum_pool(name="psum", bufs=6))
         psum_o = ctx.enter_context(tc.psum_pool(name="psum_o", bufs=2))
         ctx.enter_context(tc.manual_schedule())
 
-        W0 = WIDTHS[0]
-        WR = 1536 - W0
-        s_raw = [keep.tile([P, 2, 2048], U8, name="s_raw%d" % g, align_bytes=64) for g in range(2)]
+        s_raw = [keep.tile([P, 2, 2048], U8, name="s_raw%d" % k, align_bytes=64) for k in range(2)]
         s_sraw = keep.tile([P, G, 1024], U8, align_bytes=64)
         s_cod = [keep.tile([P, G, 2, 256], U8, name="s_cod%d" % t, align_bytes=64) for t in range(T)]
         s_sca = [keep.tile([P, G, 2, 128], U8, name="s_sca%d" % t, align_bytes=64) for t in range(T)]
-        x_cod = [keep.tile([P, G, 2 * w], U8, name="x_cod%d" % c, align_bytes=64) for c, w in enumerate(WIDTHS)]
-        x_sca0 = keep.tile([P, G, W0], U8, align_bytes=64)
-        x_scar = keep.tile([P, G, WR], U8, align_bytes=64)
+        x_cod = [keep.tile([P, G, 2 * W], U8, name="x_cod%d" % c, align_bytes=64) for c in range(CHUNKS)]
+        x_sca0 = keep.tile([P, G, W], U8, align_bytes=64)
+        x_scar = keep.tile([P, G, M - W], U8, align_bytes=64)
         c_cod = keep.tile([P, 2, 1024], U8, align_bytes=64)
         c_sca = keep.tile([P, 2, 512], U8, align_bytes=64)
         ph = keep.tile([P, T], BF16)
@@ -65,18 +77,12 @@ def tile_postfiltered_beam_combining_f2_kernel(
         cgi = keep.tile([P, T], F32)
         ndgr = keep.tile([P, T], F32)
         dgi = keep.tile([P, T], F32)
-        dummy = keep.tile([P, T], F32)
+        warm = keep.tile([P, T], F32)
+        warm1 = keep.tile([P, T], F32)
+        warm2 = keep.tile([P, T], F32)
 
         def fill_zero(eng, plane):
             eng.memset(plane[:].rearrange("p g n -> p (g n)").bitcast(I32), 0)
-
-        def x_scale(c):
-            if c == 0:
-                return x_sca0[:]
-            return x_scar[:, :, STARTS[c] - W0 : STARTS[c] - W0 + WIDTHS[c]]
-
-        fill_zero(nc.vector, s_sraw)
-        fill_zero(nc.gpsimd, x_sca0)
 
         xs_view = x_scales.rearrange("g (q r) n -> q r g n", r=4)
         ss_view = s_scales.rearrange("g (q r) n -> q r g n", r=4)
@@ -86,43 +92,46 @@ def tile_postfiltered_beam_combining_f2_kernel(
         cw_view = c_words.rearrange("g p b -> p g b")
 
         def load_x(c):
-            a = 2 * STARTS[c]
-            nc.sync.dma_start(
-                out=x_cod[c][:].bitcast(I32), in_=xw_view[:, :, a : a + 2 * WIDTHS[c]].bitcast(I32)
-            )
+            a = 2 * c * W
+            nc.sync.dma_start(out=x_cod[c][:].bitcast(I32), in_=xw_view[:, :, a : a + 2 * W].bitcast(I32))
 
         def load_rows(eng, plane, view):
             for q in range(4):
                 eng.dma_start(out=plane[32 * q : 32 * q + 4, :, :].bitcast(I32), in_=view[q].bitcast(I32))
 
+        nc.vector.memset(warm[:], 0.0)
+        fill_zero(nc.vector, s_sraw)
+        fill_zero(nc.vector, x_sca0)
         nc.gpsimd.dma_start(out=ph[:], in_=phi.rearrange("(p t) -> p t", t=T))
         nc.gpsimd.dma_start(out=nz_b[:], in_=noise.rearrange("(p t) -> p t", t=T))
         nc.gpsimd.dma_start(out=gn[:], in_=gain.rearrange("(h p t) -> p h t", h=2, t=T))
-        fill_zero(nc.gpsimd, x_scar)
-        fill_zero(nc.gpsimd, c_sca)
+        load_rows(nc.scalar, s_sraw, ss_view)
+        nc.scalar.activation(out=warm1[:], in_=warm[:], func=ACT.Sin)
         for k in range(2):
             nc.sync.dma_start(out=s_raw[k][:].bitcast(I32), in_=sw_view[:, 2 * k : 2 * k + 2, :].bitcast(I32))
-        load_rows(nc.scalar, s_sraw, ss_view)
         load_x(0)
-        load_rows(nc.sync, x_sca0, xs_view[:, :, :, 0:W0])
+        load_rows(nc.sync, x_sca0, xs_view[:, :, :, 0:W])
         load_x(1)
-        load_rows(nc.sync, x_scar, xs_view[:, :, :, W0:1536])
-        for c in range(2, CHUNKS):
-            load_x(c)
-        load_rows(nc.sync, c_sca, cs_view)
-        nc.sync.dma_start(out=c_cod[:].bitcast(I32), in_=cw_view.bitcast(I32))
 
         nc.scalar.activation(out=sd[:], in_=ph[:], func=ACT.Sin)
         nc.scalar.activation(out=sh[:], in_=ph[:], func=ACT.Sin, scale=0.5)
+        nc.scalar.activation(out=warm2[:], in_=warm[:], func=ACT.Abs_reciprocal_sqrt, bias=1.0)
         nc.gpsimd.tensor_copy(out=nz[:], in_=nz_b[:])
-        nc.scalar.activation(out=dummy[:], in_=nz[:], func=ACT.Abs_reciprocal_sqrt)
         nc.gpsimd.tensor_tensor(out=s2[:], in0=sh[:], in1=sh[:], op=MUL)
-        nc.gpsimd.tensor_scalar(out=cc[:], in0=s2[:], scalar1=-2.0, scalar2=1.0, op0=MUL, op1=ADD)
         nc.gpsimd.tensor_scalar(out=nd[:], in0=sd[:], scalar1=-1.0, scalar2=0.0, op0=MUL, op1=ADD)
+        nc.gpsimd.tensor_scalar(out=cc[:], in0=s2[:], scalar1=-2.0, scalar2=1.0, op0=MUL, op1=ADD)
         nc.gpsimd.tensor_tensor(out=ndgr[:], in0=nd[:], in1=gn[:, 0, :], op=MUL)
         nc.gpsimd.tensor_tensor(out=dgi[:], in0=sd[:], in1=gn[:, 1, :], op=MUL)
         nc.gpsimd.tensor_tensor(out=cgr[:], in0=cc[:], in1=gn[:, 0, :], op=MUL)
         nc.gpsimd.tensor_tensor(out=cgi[:], in0=cc[:], in1=gn[:, 1, :], op=MUL)
+        fill_zero(nc.gpsimd, x_scar)
+        fill_zero(nc.gpsimd, c_sca)
+
+        load_rows(nc.sync, x_scar, xs_view[:, :, :, W:M])
+        for c in range(2, CHUNKS):
+            load_x(c)
+        load_rows(nc.sync, c_sca, cs_view)
+        nc.sync.dma_start(out=c_cod[:].bitcast(I32), in_=cw_view.bitcast(I32))
 
         def permute_codes(t, k):
             nc.vector.tensor_copy(
@@ -136,14 +145,14 @@ def tile_postfiltered_beam_combining_f2_kernel(
                 in_=s_sraw[:].rearrange("p g (h m t) -> p (g h) m t", h=2, t=T)[:, :, :, t],
             )
 
-        y = [None] * PAIRS
-        sq = [None] * PAIRS
-        ab = [None] * PAIRS
-        pw = [None] * PAIRS
-        rs = [None] * PAIRS
-        r2 = [None] * PAIRS
-        uv = [None] * CHUNKS
-        ff = [None] * CHUNKS
+        y = {}
+        sq = {}
+        ab = {}
+        pw = {}
+        rs = {}
+        r2 = {}
+        uv = {}
+        ff = {}
         zt = {}
         zc = {}
         zs = {}
@@ -159,7 +168,7 @@ def tile_postfiltered_beam_combining_f2_kernel(
                         lhsT=s_cod[t][:, g, h, :].bitcast(FP4X4),
                         lhsT_scale=s_sca[t][:, g, h, :],
                         rhs=x_cod[c][:, g, :].bitcast(FP4X4),
-                        rhs_scale=x_scale(c)[:, g, :],
+                        rhs_scale=x_sca0[:, g, :] if c == 0 else x_scar[:, g, (c - 1) * W : c * W],
                         start=(g == 0),
                         stop=(g == G - 1),
                     )
@@ -169,16 +178,16 @@ def tile_postfiltered_beam_combining_f2_kernel(
             nc.scalar.activation(out=sq[j][:], in_=y[j][:], func=ACT.Square)
 
         def cross(j, h):
-            c, t = divmod(j, T)
+            t = j % T
             if h == 0:
-                ab[j] = work.tile([P, 2, W], F32, name="ab")
+                ab[j] = cross_pool.tile([P, 2, W], F32, name="ab")
             k = (ndgr, dgi)[h]
             nc.scalar.activation(out=ab[j][:, h, :], in_=y[j][:, 1 - h, :], func=ACT.Copy, scale=k[:, t : t + 1])
 
         def power(j):
-            if j % 2 == 0:
-                pw[j // 2] = work.tile([P, 2, W], F32, name="pw")
-            nc.gpsimd.tensor_tensor(out=pw[j // 2][:, j % 2, :], in0=sq[j][:, 0, :], in1=sq[j][:, 1, :], op=ADD)
+            pw[j] = (free_pool if j >= PAIRS - TAIL_FREE else power_pool).tile([P, W], F32, name="pw")
+            eng = nc.vector if j in P_ON_V else nc.gpsimd
+            eng.tensor_tensor(out=pw[j][:], in0=sq[j][:, 0, :], in1=sq[j][:, 1, :], op=ADD)
 
         def rotate(j, h):
             c, t = divmod(j, T)
@@ -191,91 +200,66 @@ def tile_postfiltered_beam_combining_f2_kernel(
 
         def inverse_root(j):
             t = j % T
-            if j % 2 == 0:
-                rs[j // 2] = work.tile([P, 2, W], F32, name="rs")
-            nc.scalar.activation(
-                out=rs[j // 2][:, j % 2, :], in_=pw[j // 2][:, j % 2, :], func=ACT.Abs_reciprocal_sqrt, bias=nz[:, t : t + 1]
-            )
+            rs[j] = work.tile([P, W], F32, name="rs")
+            nc.scalar.activation(out=rs[j][:], in_=pw[j][:], func=ACT.Abs_reciprocal_sqrt, bias=nz[:, t : t + 1])
 
-        def inverse(d):
-            r2[d] = work.tile([P, 2, W], F32, name="r2")
-            nc.scalar.activation(out=r2[d][:], in_=rs[d][:], func=ACT.Square)
+        def inverse(j):
+            r2[j] = work.tile([P, W], F32, name="r2")
+            if j in R2_ON_V:
+                nc.vector.tensor_tensor(out=r2[j][:], in0=rs[j][:], in1=rs[j][:], op=MUL)
+            elif j in R2_ON_G:
+                nc.gpsimd.tensor_tensor(out=r2[j][:], in0=rs[j][:], in1=rs[j][:], op=MUL)
+            else:
+                nc.scalar.activation(out=r2[j][:], in_=rs[j][:], func=ACT.Square)
 
-        def wiener(d):
-            c, e = divmod(d, T // 2)
-            if e == 0:
+        def wiener(j):
+            c, t = divmod(j, T)
+            if t == 0:
                 ff[c] = wide.tile([P, T, W], F32, name="ff")
-            nc.vector.tensor_tensor(out=ff[c][:, 2 * e : 2 * e + 2, :], in0=pw[d][:], in1=r2[d][:], op=MUL)
+            nc.vector.tensor_tensor(out=ff[c][:, t, :], in0=pw[j][:], in1=r2[j][:], op=MUL)
 
         def weigh(c, b, h):
-            sb = min(SB, WIDTHS[c])
             if h == 0:
-                zt[c, b] = wide.tile([P, 2, sb, T], BF16, name="zt", align_bytes=64)
-            cols = slice(b * sb, (b + 1) * sb)
+                zt[c, b] = work.tile([P, 2, P, T], BF16, name="zt", align_bytes=64)
+            cols = slice(b * P, (b + 1) * P)
             nc.vector.tensor_tensor(
-                out=zt[c, b][:, h, :, :].rearrange("p (c i) t -> p c t i", i=4),
-                in0=uv[c][:, :, h, cols].rearrange("p t (c i) -> p c t i", i=4),
-                in1=ff[c][:, :, cols].rearrange("p t (c i) -> p c t i", i=4),
+                out=zt[c, b][:, h, :, :].rearrange("p (c i) t -> p c t i", i=FI),
+                in0=uv[c][:, :, h, cols].rearrange("p t (c i) -> p c t i", i=FI),
+                in1=ff[c][:, :, cols].rearrange("p t (c i) -> p c t i", i=FI),
                 op=MUL,
             )
 
         def quantise(c, b):
-            sb = min(SB, WIDTHS[c])
-            zc[c, b] = wide.tile([P, 2, sb], U32, name="zc", align_bytes=64)
-            zs[c, b] = wide.tile([P, 2, sb], U8, name="zs", align_bytes=64)
+            zc[c, b] = work.tile([P, 2, P], U32, name="zc", align_bytes=64)
+            zs[c, b] = work.tile([P, 2, P], U8, name="zs", align_bytes=64)
             nc.vector.quantize_mx(
                 out=zc[c, b][:].rearrange("p h n -> p (h n)").bitcast(FP8X4),
                 scales=zs[c, b][:].rearrange("p h n -> p (h n)"),
                 in_=zt[c, b][:].rearrange("p h n t -> p (h n t)"),
             )
 
-        def combine(c, b, k):
+        def combine(c, b):
             o = psum_o.tile([P, 512], F32, name="o")
-            oo[c, b, k] = o
+            oo[c, b] = o
             for h in range(2):
                 nc.tensor.matmul_mx(
                     out=o[:],
-                    lhsT=zc[c, b][:, h, k * P : (k + 1) * P].bitcast(FP8X4),
-                    lhsT_scale=zs[c, b][:, h, k * P : (k + 1) * P],
+                    lhsT=zc[c, b][:, h, :].bitcast(FP8X4),
+                    lhsT_scale=zs[c, b][:, h, :],
                     rhs=c_cod[:, h, :].bitcast(FP4X4),
                     rhs_scale=c_sca[:, h, :],
                     start=(h == 0),
                     stop=(h == 1),
                 )
 
-        def store(c, b, k):
-            sb = min(SB, WIDTHS[c])
-            r0 = STARTS[c] + b * sb + k * P
+        def store(c, b):
+            r0 = c * W + b * P
             res = work.tile([P, 512], F32, name="res")
-            if (r0 // P) % O_MOD in O_ON_S:
-                nc.scalar.copy(out=res[:], in_=oo[c, b, k][:])
+            if r0 // P in O_ON_S:
+                nc.scalar.copy(out=res[:], in_=oo[c, b][:])
             else:
-                nc.vector.tensor_copy(out=res[:], in_=oo[c, b, k][:])
+                nc.vector.tensor_copy(out=res[:], in_=oo[c, b][:])
             nc.sync.dma_start(out=out[r0 : r0 + P, :], in_=res[:])
-
-        v_queue = []
-        pe_queue = []
-        o_queue = []
-
-        def chunk_done(c):
-            sb = min(SB, WIDTHS[c])
-            nb = WIDTHS[c] // sb
-            for b in range(nb):
-                v_queue.append(("F", c, b, 0))
-                if b > 0:
-                    v_queue.append(("Q", c, b - 1, 0))
-                v_queue.append(("F", c, b, 1))
-            v_queue.append(("Q", c, nb - 1, 0))
-
-        def v_pop(n):
-            for i in range(min(n, len(v_queue))):
-                kind, c, b, h = v_queue.pop(0)
-                if kind == "F":
-                    weigh(c, b, h)
-                else:
-                    quantise(c, b)
-                    for k in range(min(SB, WIDTHS[c]) // P):
-                        pe_queue.append((c, b, k))
 
         permute_codes(0, 0)
         permute_scales(0)
@@ -283,40 +267,60 @@ def tile_postfiltered_beam_combining_f2_kernel(
         permute_codes(1, 0)
         permute_codes(1, 1)
         permute_scales(1)
-        steer(0)
-        for j in range(PAIRS + 12):
+        for j in range(AHEAD):
+            steer(j)
+        fq = []
+        qq = []
+        cq = []
+        oq = []
+        for j in range(PAIRS + 14):
+            tail = j >= PAIRS
             if j + 2 < T:
                 permute_codes(j + 2, 0)
                 permute_codes(j + 2, 1)
                 permute_scales(j + 2)
-            for i in (2 * j + 1, 2 * j + 2) if j == 0 else (j + 2,):
-                if i < PAIRS:
-                    steer(i)
-            for i in range(min(2, len(pe_queue))):
-                key = pe_queue.pop(0)
-                combine(*key)
-                o_queue.append(key)
+            if j + AHEAD < PAIRS:
+                steer(j + AHEAD)
+            while cq and cq[0][0] <= j:
+                k = cq.pop(0)[1:]
+                combine(*k)
+                oq.append((j + O_LAG,) + k)
             if j < PAIRS:
                 square(j)
-                power(j)
-            if 0 < j <= PAIRS:
-                inverse_root(j - 1)
+            if 0 <= j - ARS_LAG < PAIRS:
+                inverse_root(j - ARS_LAG)
             if j < PAIRS:
                 cross(j, 0)
-            if 0 < j <= PAIRS and j % 2 == 0:
-                inverse(j // 2 - 1)
+            if 0 <= j - ARS_LAG < PAIRS:
+                inverse(j - ARS_LAG)
             if j < PAIRS:
                 cross(j, 1)
-            if 0 < j <= PAIRS:
-                rotate(j - 1, 0)
-                rotate(j - 1, 1)
-            if 1 < j <= PAIRS + 1 and j % 2 == 1:
-                wiener(j // 2 - 1)
-                if (j - 2) % T == T - 1:
-                    chunk_done((j - 2) // T)
-            n = 1 if j < PAIRS else 2
-            while n > 0 and v_queue:
-                n -= v_queue[0][0] == "F"
-                v_pop(1)
-            while len(o_queue) > (0 if j > PAIRS else 2):
-                store(*o_queue.pop(0))
+            if 0 <= j - WIEN_LAG < PAIRS:
+                wiener(j - WIEN_LAG)
+                if (j - WIEN_LAG) % T == T - 1:
+                    c = (j - WIEN_LAG) // T
+                    fq += [(c, 0, 0), (c, 0, 1), (c, 1, 0), (c, 1, 1)]
+            for i in [j - P_LAG] if j < PAIRS - TAIL_FREE + P_LAG else []:
+                if 0 <= i < PAIRS - TAIL_FREE:
+                    power(i)
+            if PAIRS - TAIL_FREE <= j < PAIRS:
+                power(j)
+            if 0 <= j - ROT_LAG < PAIRS:
+                rotate(j - ROT_LAG, 0)
+                rotate(j - ROT_LAG, 1)
+            while qq and (qq[0][0] < j):
+                k = qq.pop(0)[1:]
+                quantise(*k)
+                cq.append((j + C_LAG,) + k)
+            for i in range(4 if j >= PAIRS + WIEN_LAG - 1 else F_STEP):
+                if fq:
+                    c, b, h = fq.pop(0)
+                    weigh(c, b, h)
+                    if h == 1:
+                        qq.append((j - (1 if tail else 0), c, b))
+                    if tail and qq and len(fq) % 2 == 1:
+                        k = qq.pop(0)[1:]
+                        quantise(*k)
+                        cq.append((j, ) + k)
+            while oq and oq[0][0] <= j:
+                store(*oq.pop(0)[1:])

@@ -1,5 +1,7 @@
 from contextlib import ExitStack
 
+import math
+
 import concourse.mybir as mybir
 
 FLOPS = 2 * 1536 * 2048 * 1024 + 2 * 1536 * 1024 * 512
@@ -19,49 +21,47 @@ P = 128
 G = 4
 T = 4
 M = 1536
-W = 256
-CHUNKS = M // W
-PAIRS = CHUNKS * T
-O_ON_S = [0, 2, 4, 6, 8, 10, 11]
-P_ON_V = []
-R2_ON_V = []
-R2_ON_G = []
-TAIL_FREE = 0
-PW_BUFS = 3
-AB_BUFS = 3
-P_LAG = 1
-ARS_LAG = 2
+WIDTHS = [256, 512, 512, 256]
+O_ON_S = [0, 1, 2, 3, 4, 5, 6, 7, 8, 9, 10, 11]
+P_ON_G = []
+ARS_LAG = 1
 ROT_LAG = 1
-WIEN_LAG = 3
+WIEN_LAG = 2
 C_LAG = 1
-O_LAG = 1
-AHEAD = 2
-F_STEP = 1
-FI = 2
+O_LAG = 0
+AHEAD = 1
+FI = 4
+FB = 256
+FB_LAST = 128
+BUFS = 4
+TINY = 1.3e-18
+O_BUFS = 2
+F_FIRST = 1
 
 
 def tile_postfiltered_beam_combining_f2_kernel(
     tc, x_words, x_scales, s_words, s_scales, phi, noise, gain, c_words, c_scales, out
 ):
     nc = tc.nc
+    CH = len(WIDTHS)
+    PAIRS = CH * T
+    START = [sum(WIDTHS[:c]) for c in range(CH)]
+    W0 = WIDTHS[0]
     with ExitStack() as ctx:
         keep = ctx.enter_context(tc.tile_pool(name="keep", bufs=1))
-        work = ctx.enter_context(tc.tile_pool(name="work", bufs=3))
-        cross_pool = ctx.enter_context(tc.tile_pool(name="cross", bufs=AB_BUFS))
-        power_pool = ctx.enter_context(tc.tile_pool(name="power", bufs=PW_BUFS))
-        free_pool = ctx.enter_context(tc.tile_pool(name="free", bufs=4))
+        work = ctx.enter_context(tc.tile_pool(name="work", bufs=BUFS))
         wide = ctx.enter_context(tc.tile_pool(name="wide", bufs=3))
-        psum = ctx.enter_context(tc.psum_pool(name="psum", bufs=6))
-        psum_o = ctx.enter_context(tc.psum_pool(name="psum_o", bufs=2))
+        psum = ctx.enter_context(tc.psum_pool(name="psum", bufs=8 - O_BUFS))
+        psum_o = ctx.enter_context(tc.psum_pool(name="psum_o", bufs=O_BUFS))
         ctx.enter_context(tc.manual_schedule())
 
-        s_raw = [keep.tile([P, 2, 2048], U8, name="s_raw%d" % k, align_bytes=64) for k in range(2)]
+        s_raw = keep.tile([P, G, 2048], U8, align_bytes=64)
         s_sraw = keep.tile([P, G, 1024], U8, align_bytes=64)
         s_cod = [keep.tile([P, G, 2, 256], U8, name="s_cod%d" % t, align_bytes=64) for t in range(T)]
         s_sca = [keep.tile([P, G, 2, 128], U8, name="s_sca%d" % t, align_bytes=64) for t in range(T)]
-        x_cod = [keep.tile([P, G, 2 * W], U8, name="x_cod%d" % c, align_bytes=64) for c in range(CHUNKS)]
-        x_sca0 = keep.tile([P, G, W], U8, align_bytes=64)
-        x_scar = keep.tile([P, G, M - W], U8, align_bytes=64)
+        x_cod = [keep.tile([P, G, 2 * w], U8, name="x_cod%d" % c, align_bytes=64) for c, w in enumerate(WIDTHS)]
+        x_sca0 = keep.tile([P, G, W0], U8, align_bytes=64)
+        x_scar = keep.tile([P, G, M - W0], U8, align_bytes=64)
         c_cod = keep.tile([P, 2, 1024], U8, align_bytes=64)
         c_sca = keep.tile([P, 2, 512], U8, align_bytes=64)
         ph = keep.tile([P, T], BF16)
@@ -70,13 +70,16 @@ def tile_postfiltered_beam_combining_f2_kernel(
         nz = keep.tile([P, T], F32)
         sd = keep.tile([P, T], F32)
         sh = keep.tile([P, T], F32)
-        s2 = keep.tile([P, T], F32)
-        cc = keep.tile([P, T], F32)
-        nd = keep.tile([P, T], F32)
-        cgr = keep.tile([P, T], F32)
-        cgi = keep.tile([P, T], F32)
-        ndgr = keep.tile([P, T], F32)
-        dgi = keep.tile([P, T], F32)
+        shsq = keep.tile([P, T], F32)
+        den = keep.tile([P, 3, T], F32)
+        inv = keep.tile([P, 3, T], F32)
+        rat = keep.tile([P, T], F32)
+        ratc = keep.tile([P, T], F32)
+        dg = keep.tile([P, T], F32)
+        k_r = keep.tile([P, T], F32)
+        k_i = keep.tile([P, T], F32)
+        k_u = keep.tile([P, T], F32)
+        kap = keep.tile([P, T], F32)
         warm = keep.tile([P, T], F32)
         warm1 = keep.tile([P, T], F32)
         warm2 = keep.tile([P, T], F32)
@@ -88,12 +91,11 @@ def tile_postfiltered_beam_combining_f2_kernel(
         ss_view = s_scales.rearrange("g (q r) n -> q r g n", r=4)
         cs_view = c_scales.rearrange("g (q r) n -> q r g n", r=4)
         xw_view = x_words.rearrange("g p b -> p g b")
-        sw_view = s_words.rearrange("g p b -> p g b")
         cw_view = c_words.rearrange("g p b -> p g b")
 
         def load_x(c):
-            a = 2 * c * W
-            nc.sync.dma_start(out=x_cod[c][:].bitcast(I32), in_=xw_view[:, :, a : a + 2 * W].bitcast(I32))
+            a = 2 * START[c]
+            nc.sync.dma_start(out=x_cod[c][:].bitcast(I32), in_=xw_view[:, :, a : a + 2 * WIDTHS[c]].bitcast(I32))
 
         def load_rows(eng, plane, view):
             for q in range(4):
@@ -107,36 +109,31 @@ def tile_postfiltered_beam_combining_f2_kernel(
         nc.gpsimd.dma_start(out=gn[:], in_=gain.rearrange("(h p t) -> p h t", h=2, t=T))
         load_rows(nc.scalar, s_sraw, ss_view)
         nc.scalar.activation(out=warm1[:], in_=warm[:], func=ACT.Sin)
-        for k in range(2):
-            nc.sync.dma_start(out=s_raw[k][:].bitcast(I32), in_=sw_view[:, 2 * k : 2 * k + 2, :].bitcast(I32))
+        sw_view = s_words.rearrange("g p b -> p g b")
+        for g0, g1 in ((0, 1), (1, 4)):
+            nc.sync.dma_start(out=s_raw[:, g0:g1, :].bitcast(I32), in_=sw_view[:, g0:g1, :].bitcast(I32))
         load_x(0)
-        load_rows(nc.sync, x_sca0, xs_view[:, :, :, 0:W])
+        load_rows(nc.sync, x_sca0, xs_view[:, :, :, 0:W0])
         load_x(1)
 
         nc.scalar.activation(out=sd[:], in_=ph[:], func=ACT.Sin)
         nc.scalar.activation(out=sh[:], in_=ph[:], func=ACT.Sin, scale=0.5)
+        nc.scalar.activation(out=shsq[:], in_=sh[:], func=ACT.Square, scale=math.sqrt(2.0))
+        nc.scalar.activation(out=den[:, 0, :], in_=shsq[:], func=ACT.Copy, scale=-1.0, bias=1.0)
         nc.scalar.activation(out=warm2[:], in_=warm[:], func=ACT.Abs_reciprocal_sqrt, bias=1.0)
-        nc.gpsimd.tensor_copy(out=nz[:], in_=nz_b[:])
-        nc.gpsimd.tensor_tensor(out=s2[:], in0=sh[:], in1=sh[:], op=MUL)
-        nc.gpsimd.tensor_scalar(out=nd[:], in0=sd[:], scalar1=-1.0, scalar2=0.0, op0=MUL, op1=ADD)
-        nc.gpsimd.tensor_scalar(out=cc[:], in0=s2[:], scalar1=-2.0, scalar2=1.0, op0=MUL, op1=ADD)
-        nc.gpsimd.tensor_tensor(out=ndgr[:], in0=nd[:], in1=gn[:, 0, :], op=MUL)
-        nc.gpsimd.tensor_tensor(out=dgi[:], in0=sd[:], in1=gn[:, 1, :], op=MUL)
-        nc.gpsimd.tensor_tensor(out=cgr[:], in0=cc[:], in1=gn[:, 0, :], op=MUL)
-        nc.gpsimd.tensor_tensor(out=cgi[:], in0=cc[:], in1=gn[:, 1, :], op=MUL)
         fill_zero(nc.gpsimd, x_scar)
         fill_zero(nc.gpsimd, c_sca)
 
-        load_rows(nc.sync, x_scar, xs_view[:, :, :, W:M])
-        for c in range(2, CHUNKS):
+        load_rows(nc.sync, x_scar, xs_view[:, :, :, W0:M])
+        for c in range(2, CH):
             load_x(c)
         load_rows(nc.sync, c_sca, cs_view)
         nc.sync.dma_start(out=c_cod[:].bitcast(I32), in_=cw_view.bitcast(I32))
 
-        def permute_codes(t, k):
+        def permute_codes(t, g, n):
             nc.vector.tensor_copy(
-                out=s_cod[t][:, 2 * k : 2 * k + 2, :, :].rearrange("p g h (m e) -> p (g h) m e", e=2),
-                in_=s_raw[k][:].rearrange("p g (h m t e) -> p (g h) m t e", h=2, t=T, e=2)[:, :, :, t, :],
+                out=s_cod[t][:, g : g + n, :, :].rearrange("p g h (m e) -> p (g h) m e", e=2),
+                in_=s_raw[:, g : g + n, :].rearrange("p g (h m t e) -> p (g h) m t e", h=2, t=T, e=2)[:, :, :, t, :],
             )
 
         def permute_scales(t):
@@ -158,70 +155,88 @@ def tile_postfiltered_beam_combining_f2_kernel(
         zs = {}
         oo = {}
 
+        def fb(c):
+            return min(FB if c < CH - 1 else FB_LAST, WIDTHS[c])
+
+        def width(j):
+            return WIDTHS[j // T]
+
         def steer(j):
             c, t = divmod(j, T)
-            y[j] = psum.tile([P, 2, W], F32, name="y")
+            w = WIDTHS[c]
+            if w == 512:
+                yr = psum.tile([P, 512], F32, name="y")
+                yi = psum.tile([P, 512], F32, name="y")
+                y[j] = (yr[:], yi[:])
+            else:
+                yy = psum.tile([P, 2, w], F32, name="y")
+                y[j] = (yy[:, 0, :], yy[:, 1, :], yy[:])
             for h in range(2):
                 for g in range(G):
                     nc.tensor.matmul_mx(
-                        out=y[j][:, h, :],
+                        out=y[j][h],
                         lhsT=s_cod[t][:, g, h, :].bitcast(FP4X4),
                         lhsT_scale=s_sca[t][:, g, h, :],
                         rhs=x_cod[c][:, g, :].bitcast(FP4X4),
-                        rhs_scale=x_sca0[:, g, :] if c == 0 else x_scar[:, g, (c - 1) * W : c * W],
+                        rhs_scale=x_sca0[:, g, :] if c == 0 else x_scar[:, g, START[c] - W0 : START[c] - W0 + w],
                         start=(g == 0),
                         stop=(g == G - 1),
                     )
 
         def square(j):
-            sq[j] = work.tile([P, 2, W], F32, name="sq")
-            nc.scalar.activation(out=sq[j][:], in_=y[j][:], func=ACT.Square)
+            w = width(j)
+            sq[j] = work.tile([P, 2, w], F32, name="sq")
+            if w == 512:
+                for h in range(2):
+                    nc.scalar.activation(out=sq[j][:, h, :], in_=y[j][h], func=ACT.Square)
+            else:
+                nc.scalar.activation(out=sq[j][:], in_=y[j][2], func=ACT.Square)
 
-        def cross(j, h):
+        def cross(j):
             t = j % T
-            if h == 0:
-                ab[j] = cross_pool.tile([P, 2, W], F32, name="ab")
-            k = (ndgr, dgi)[h]
-            nc.scalar.activation(out=ab[j][:, h, :], in_=y[j][:, 1 - h, :], func=ACT.Copy, scale=k[:, t : t + 1])
+            ab[j] = work.tile([P, width(j)], F32, name="ab")
+            nc.scalar.activation(out=ab[j][:], in_=y[j][1], func=ACT.Copy, scale=k_i[:, t : t + 1])
 
         def power(j):
-            pw[j] = (free_pool if j >= PAIRS - TAIL_FREE else power_pool).tile([P, W], F32, name="pw")
-            eng = nc.vector if j in P_ON_V else nc.gpsimd
+            pw[j] = work.tile([P, width(j)], F32, name="pw")
+            eng = nc.gpsimd if j in P_ON_G else nc.vector
             eng.tensor_tensor(out=pw[j][:], in0=sq[j][:, 0, :], in1=sq[j][:, 1, :], op=ADD)
 
         def rotate(j, h):
             c, t = divmod(j, T)
             if t == 0 and h == 0:
-                uv[c] = wide.tile([P, T, 2, W], F32, name="uv")
-            k = (cgr, cgi)[h]
-            nc.vector.scalar_tensor_tensor(
-                out=uv[c][:, t, h, :], in0=y[j][:, h, :], scalar=k[:, t : t + 1], in1=ab[j][:, h, :], op0=MUL, op1=ADD
-            )
+                uv[c] = wide.tile([P, T, 2, width(j)], F32, name="uv")
+            if h == 0:
+                nc.vector.scalar_tensor_tensor(
+                    out=uv[c][:, t, 0, :], in0=y[j][0], scalar=k_r[:, t : t + 1], in1=ab[j][:], op0=MUL, op1=ADD
+                )
+            else:
+                nc.vector.scalar_tensor_tensor(
+                    out=uv[c][:, t, 1, :], in0=uv[c][:, t, 0, :], scalar=k_u[:, t : t + 1], in1=y[j][1], op0=MUL, op1=ADD
+                )
 
         def inverse_root(j):
             t = j % T
-            rs[j] = work.tile([P, W], F32, name="rs")
+            rs[j] = work.tile([P, width(j)], F32, name="rs")
             nc.scalar.activation(out=rs[j][:], in_=pw[j][:], func=ACT.Abs_reciprocal_sqrt, bias=nz[:, t : t + 1])
 
         def inverse(j):
-            r2[j] = work.tile([P, W], F32, name="r2")
-            if j in R2_ON_V:
-                nc.vector.tensor_tensor(out=r2[j][:], in0=rs[j][:], in1=rs[j][:], op=MUL)
-            elif j in R2_ON_G:
-                nc.gpsimd.tensor_tensor(out=r2[j][:], in0=rs[j][:], in1=rs[j][:], op=MUL)
-            else:
-                nc.scalar.activation(out=r2[j][:], in_=rs[j][:], func=ACT.Square)
+            r2[j] = work.tile([P, width(j)], F32, name="r2")
+            nc.scalar.activation(out=r2[j][:], in_=rs[j][:], func=ACT.Square)
 
         def wiener(j):
             c, t = divmod(j, T)
             if t == 0:
-                ff[c] = wide.tile([P, T, W], F32, name="ff")
-            nc.vector.tensor_tensor(out=ff[c][:, t, :], in0=pw[j][:], in1=r2[j][:], op=MUL)
+                ff[c] = wide.tile([P, T, width(j)], F32, name="ff")
+            nc.vector.scalar_tensor_tensor(
+                out=ff[c][:, t, :], in0=pw[j][:], scalar=kap[:, t : t + 1], in1=r2[j][:], op0=MUL, op1=MUL
+            )
 
         def weigh(c, b, h):
+            n = fb(c)
             if h == 0:
-                zt[c, b] = work.tile([P, 2, P, T], BF16, name="zt", align_bytes=64)
-            cols = slice(b * P, (b + 1) * P)
+                zt[c, b] = work.tile([P, 2, n, T], BF16, name="zt", align_bytes=64)
+            cols = slice(b * n, (b + 1) * n)
             nc.vector.tensor_tensor(
                 out=zt[c, b][:, h, :, :].rearrange("p (c i) t -> p c t i", i=FI),
                 in0=uv[c][:, :, h, cols].rearrange("p t (c i) -> p c t i", i=FI),
@@ -230,59 +245,69 @@ def tile_postfiltered_beam_combining_f2_kernel(
             )
 
         def quantise(c, b):
-            zc[c, b] = work.tile([P, 2, P], U32, name="zc", align_bytes=64)
-            zs[c, b] = work.tile([P, 2, P], U8, name="zs", align_bytes=64)
+            n = fb(c)
+            zc[c, b] = work.tile([P, 2, n], U32, name="zc", align_bytes=64)
+            zs[c, b] = work.tile([P, 2, n], U8, name="zs", align_bytes=64)
             nc.vector.quantize_mx(
                 out=zc[c, b][:].rearrange("p h n -> p (h n)").bitcast(FP8X4),
                 scales=zs[c, b][:].rearrange("p h n -> p (h n)"),
                 in_=zt[c, b][:].rearrange("p h n t -> p (h n t)"),
             )
 
-        def combine(c, b):
+        def combine(c, b, k):
             o = psum_o.tile([P, 512], F32, name="o")
-            oo[c, b] = o
+            oo[c, b, k] = o
             for h in range(2):
                 nc.tensor.matmul_mx(
                     out=o[:],
-                    lhsT=zc[c, b][:, h, :].bitcast(FP8X4),
-                    lhsT_scale=zs[c, b][:, h, :],
+                    lhsT=zc[c, b][:, h, k * P : (k + 1) * P].bitcast(FP8X4),
+                    lhsT_scale=zs[c, b][:, h, k * P : (k + 1) * P],
                     rhs=c_cod[:, h, :].bitcast(FP4X4),
                     rhs_scale=c_sca[:, h, :],
                     start=(h == 0),
                     stop=(h == 1),
                 )
 
-        def store(c, b):
-            r0 = c * W + b * P
+        def store(c, b, k):
+            r0 = START[c] + b * fb(c) + k * P
             res = work.tile([P, 512], F32, name="res")
             if r0 // P in O_ON_S:
-                nc.scalar.copy(out=res[:], in_=oo[c, b][:])
+                nc.scalar.copy(out=res[:], in_=oo[c, b, k][:])
             else:
-                nc.vector.tensor_copy(out=res[:], in_=oo[c, b][:])
+                nc.vector.tensor_copy(out=res[:], in_=oo[c, b, k][:])
             nc.sync.dma_start(out=out[r0 : r0 + P, :], in_=res[:])
 
-        permute_codes(0, 0)
+        permute_codes(0, 0, 1)
         permute_scales(0)
-        permute_codes(0, 1)
-        permute_codes(1, 0)
-        permute_codes(1, 1)
+        permute_codes(0, 1, 3)
+        nc.vector.tensor_scalar(out=den[:, 1:3, :], in0=gn[:], scalar1=TINY, scalar2=None, op0=ADD)
+        permute_codes(1, 0, 2)
+        nc.vector.reciprocal(out=inv[:], in_=den[:])
+        nc.vector.tensor_copy(out=nz[:], in_=nz_b[:])
+        permute_codes(1, 2, 2)
+        nc.vector.tensor_tensor(out=rat[:], in0=den[:, 1, :], in1=inv[:, 2, :], op=MUL)
+        nc.vector.tensor_tensor(out=kap[:], in0=den[:, 2, :], in1=inv[:, 0, :], op=MUL)
+        nc.vector.tensor_tensor(out=dg[:], in0=sd[:], in1=inv[:, 1, :], op=MUL)
+        nc.vector.tensor_tensor(out=ratc[:], in0=rat[:], in1=den[:, 0, :], op=MUL)
         permute_scales(1)
+        nc.vector.scalar_tensor_tensor(out=k_i[:], in0=ratc[:], scalar=-1.0, in1=sd[:], op0=MUL, op1=MUL)
+        nc.vector.tensor_tensor(out=k_r[:], in0=ratc[:], in1=den[:, 0, :], op=MUL)
+        nc.vector.tensor_tensor(out=k_u[:], in0=kap[:], in1=dg[:], op=MUL)
         for j in range(AHEAD):
             steer(j)
         fq = []
         qq = []
         cq = []
         oq = []
-        for j in range(PAIRS + 14):
+        nf = 0
+        for j in range(PAIRS + 20):
             tail = j >= PAIRS
-            if j + 2 < T:
-                permute_codes(j + 2, 0)
-                permute_codes(j + 2, 1)
-                permute_scales(j + 2)
             if j + AHEAD < PAIRS:
                 steer(j + AHEAD)
             while cq and cq[0][0] <= j:
                 k = cq.pop(0)[1:]
+                while len(oq) >= O_BUFS:
+                    store(*oq.pop(0)[1:])
                 combine(*k)
                 oq.append((j + O_LAG,) + k)
             if j < PAIRS:
@@ -290,37 +315,46 @@ def tile_postfiltered_beam_combining_f2_kernel(
             if 0 <= j - ARS_LAG < PAIRS:
                 inverse_root(j - ARS_LAG)
             if j < PAIRS:
-                cross(j, 0)
+                cross(j)
             if 0 <= j - ARS_LAG < PAIRS:
                 inverse(j - ARS_LAG)
-            if j < PAIRS:
-                cross(j, 1)
+            if 0 <= j - ROT_LAG < PAIRS:
+                rotate(j - ROT_LAG, 0)
+
+            def weigh_some(n):
+                for i in range(n):
+                    if fq:
+                        c, b, h = fq.pop(0)
+                        weigh(c, b, h)
+                        if h == 1:
+                            qq.append((j - (1 if tail else 0), c, b))
+                        if tail and qq and h == 0:
+                            quantise_one()
+
+            def quantise_one():
+                c, b = qq.pop(0)[1:]
+                quantise(c, b)
+                for k in range(fb(c) // P):
+                    cq.append((j + (0 if tail else C_LAG), c, b, k))
+
+            while qq and (qq[0][0] < j):
+                quantise_one()
             if 0 <= j - WIEN_LAG < PAIRS:
                 wiener(j - WIEN_LAG)
                 if (j - WIEN_LAG) % T == T - 1:
                     c = (j - WIEN_LAG) // T
-                    fq += [(c, 0, 0), (c, 0, 1), (c, 1, 0), (c, 1, 1)]
-            for i in [j - P_LAG] if j < PAIRS - TAIL_FREE + P_LAG else []:
-                if 0 <= i < PAIRS - TAIL_FREE:
-                    power(i)
-            if PAIRS - TAIL_FREE <= j < PAIRS:
-                power(j)
+                    n = fb(c)
+                    nf = -(-2 * (WIDTHS[c] // n) // T)
+                    for b in range(WIDTHS[c] // n):
+                        fq += [(c, b, 0), (c, b, 1)]
             if 0 <= j - ROT_LAG < PAIRS:
-                rotate(j - ROT_LAG, 0)
                 rotate(j - ROT_LAG, 1)
-            while qq and (qq[0][0] < j):
-                k = qq.pop(0)[1:]
-                quantise(*k)
-                cq.append((j + C_LAG,) + k)
-            for i in range(4 if j >= PAIRS + WIEN_LAG - 1 else F_STEP):
-                if fq:
-                    c, b, h = fq.pop(0)
-                    weigh(c, b, h)
-                    if h == 1:
-                        qq.append((j - (1 if tail else 0), c, b))
-                    if tail and qq and len(fq) % 2 == 1:
-                        k = qq.pop(0)[1:]
-                        quantise(*k)
-                        cq.append((j, ) + k)
+            weigh_some(min(nf, F_FIRST))
+            if j < PAIRS:
+                power(j)
+            if j + 2 < T:
+                permute_codes(j + 2, 0, 4)
+                permute_scales(j + 2)
+            weigh_some(2 if tail else nf - min(nf, F_FIRST))
             while oq and oq[0][0] <= j:
                 store(*oq.pop(0)[1:])

@@ -21,19 +21,21 @@ P = 128
 G = 4
 T = 4
 M = 1536
-WIDTHS = [256, 512, 512, 256]
+WIDTHS = [512,512,512]
 O_ON_S = [0, 1, 2, 3, 4, 5, 6, 7, 8, 9, 10, 11]
-P_ON_G = []
-ARS_LAG = 1
+G_COLS = 384
+P_LAG = 1
+ROT1_LAG = 2
+ARS_LAG = 2
 ROT_LAG = 1
-WIEN_LAG = 2
+WIEN_LAG = 3
 C_LAG = 1
 O_LAG = 0
 AHEAD = 1
 FI = 4
 FB = 256
 FB_LAST = 128
-BUFS = 4
+BUFS = 5
 TINY = 1.3e-18
 O_BUFS = 2
 F_FIRST = 1
@@ -50,6 +52,7 @@ def tile_postfiltered_beam_combining_f2_kernel(
     with ExitStack() as ctx:
         keep = ctx.enter_context(tc.tile_pool(name="keep", bufs=1))
         work = ctx.enter_context(tc.tile_pool(name="work", bufs=BUFS))
+        gated = ctx.enter_context(tc.tile_pool(name="gated", bufs=2))
         wide = ctx.enter_context(tc.tile_pool(name="wide", bufs=3))
         psum = ctx.enter_context(tc.psum_pool(name="psum", bufs=8 - O_BUFS))
         psum_o = ctx.enter_context(tc.psum_pool(name="psum_o", bufs=O_BUFS))
@@ -198,9 +201,15 @@ def tile_postfiltered_beam_combining_f2_kernel(
             nc.scalar.activation(out=ab[j][:], in_=y[j][1], func=ACT.Copy, scale=k_i[:, t : t + 1])
 
         def power(j):
-            pw[j] = work.tile([P, width(j)], F32, name="pw")
-            eng = nc.gpsimd if j in P_ON_G else nc.vector
-            eng.tensor_tensor(out=pw[j][:], in0=sq[j][:, 0, :], in1=sq[j][:, 1, :], op=ADD)
+            w = width(j)
+            if w == 512 and G_COLS:
+                pw[j] = gated.tile([P, w], F32, name="pwg")
+                parts = ((nc.gpsimd, 0, G_COLS), (nc.vector, G_COLS, w))
+            else:
+                pw[j] = work.tile([P, w], F32, name="pw")
+                parts = ((nc.vector, 0, w),)
+            for eng, a, b in parts:
+                eng.tensor_tensor(out=pw[j][:, a:b], in0=sq[j][:, 0, a:b], in1=sq[j][:, 1, a:b], op=ADD)
 
         def rotate(j, h):
             c, t = divmod(j, T)
@@ -302,8 +311,6 @@ def tile_postfiltered_beam_combining_f2_kernel(
         nf = 0
         for j in range(PAIRS + 20):
             tail = j >= PAIRS
-            if j + AHEAD < PAIRS:
-                steer(j + AHEAD)
             while cq and cq[0][0] <= j:
                 k = cq.pop(0)[1:]
                 while len(oq) >= O_BUFS:
@@ -318,8 +325,18 @@ def tile_postfiltered_beam_combining_f2_kernel(
                 cross(j)
             if 0 <= j - ARS_LAG < PAIRS:
                 inverse(j - ARS_LAG)
+            if 0 <= j - WIEN_LAG < PAIRS:
+                wiener(j - WIEN_LAG)
+                if (j - WIEN_LAG) % T == T - 1:
+                    c = (j - WIEN_LAG) // T
+                    n = fb(c)
+                    nf = -(-2 * (WIDTHS[c] // n) // T)
+                    for b in range(WIDTHS[c] // n):
+                        fq += [(c, b, 0), (c, b, 1)]
             if 0 <= j - ROT_LAG < PAIRS:
                 rotate(j - ROT_LAG, 0)
+            if 0 <= j - ROT1_LAG < PAIRS:
+                rotate(j - ROT1_LAG, 1)
 
             def weigh_some(n):
                 for i in range(n):
@@ -339,22 +356,14 @@ def tile_postfiltered_beam_combining_f2_kernel(
 
             while qq and (qq[0][0] < j):
                 quantise_one()
-            if 0 <= j - WIEN_LAG < PAIRS:
-                wiener(j - WIEN_LAG)
-                if (j - WIEN_LAG) % T == T - 1:
-                    c = (j - WIEN_LAG) // T
-                    n = fb(c)
-                    nf = -(-2 * (WIDTHS[c] // n) // T)
-                    for b in range(WIDTHS[c] // n):
-                        fq += [(c, b, 0), (c, b, 1)]
-            if 0 <= j - ROT_LAG < PAIRS:
-                rotate(j - ROT_LAG, 1)
-            weigh_some(min(nf, F_FIRST))
-            if j < PAIRS:
-                power(j)
+            weigh_some(nf if tail else min(nf, F_FIRST))
+            if 0 <= j - P_LAG < PAIRS:
+                power(j - P_LAG)
             if j + 2 < T:
                 permute_codes(j + 2, 0, 4)
                 permute_scales(j + 2)
             weigh_some(2 if tail else nf - min(nf, F_FIRST))
+            if j + AHEAD < PAIRS:
+                steer(j + AHEAD)
             while oq and oq[0][0] <= j:
                 store(*oq.pop(0)[1:])

@@ -23,8 +23,12 @@ T = 4
 M = 1536
 WIDTHS = [512,512,512]
 O_ON_S = [0, 1, 2, 3, 4, 5, 6, 7, 8, 9, 10, 11]
-G_COLS = 384
+G_COLS = [384, 384, 384]
 P_LAG = 1
+G_MIN = 512
+A_ON_V = 0
+R2_ON_V = [0,1,2,3]
+R2_LAG = 2
 ROT1_LAG = 2
 ARS_LAG = 2
 ROT_LAG = 1
@@ -100,23 +104,27 @@ def tile_postfiltered_beam_combining_f2_kernel(
             a = 2 * START[c]
             nc.sync.dma_start(out=x_cod[c][:].bitcast(I32), in_=xw_view[:, :, a : a + 2 * WIDTHS[c]].bitcast(I32))
 
-        def load_rows(eng, plane, view):
-            for q in range(4):
+        def load_rows(eng, plane, view, quarters=range(4)):
+            for q in quarters:
                 eng.dma_start(out=plane[32 * q : 32 * q + 4, :, :].bitcast(I32), in_=view[q].bitcast(I32))
 
         nc.vector.memset(warm[:], 0.0)
         fill_zero(nc.vector, s_sraw)
         fill_zero(nc.vector, x_sca0)
         nc.gpsimd.dma_start(out=ph[:], in_=phi.rearrange("(p t) -> p t", t=T))
-        nc.gpsimd.dma_start(out=nz_b[:], in_=noise.rearrange("(p t) -> p t", t=T))
         nc.gpsimd.dma_start(out=gn[:], in_=gain.rearrange("(h p t) -> p h t", h=2, t=T))
+        nc.gpsimd.dma_start(out=nz_b[:], in_=noise.rearrange("(p t) -> p t", t=T))
         load_rows(nc.scalar, s_sraw, ss_view)
         nc.scalar.activation(out=warm1[:], in_=warm[:], func=ACT.Sin)
         sw_view = s_words.rearrange("g p b -> p g b")
-        for g0, g1 in ((0, 1), (1, 4)):
-            nc.sync.dma_start(out=s_raw[:, g0:g1, :].bitcast(I32), in_=sw_view[:, g0:g1, :].bitcast(I32))
+        def load_s(g):
+            nc.sync.dma_start(out=s_raw[:, g : g + 2, :].bitcast(I32), in_=sw_view[:, g : g + 2, :].bitcast(I32))
+
+        load_s(0)
+        load_rows(nc.sync, x_sca0, xs_view[:, :, :, 0:W0], (0,))
+        load_s(2)
         load_x(0)
-        load_rows(nc.sync, x_sca0, xs_view[:, :, :, 0:W0])
+        load_rows(nc.sync, x_sca0, xs_view[:, :, :, 0:W0], (1, 2, 3))
         load_x(1)
 
         nc.scalar.activation(out=sd[:], in_=ph[:], func=ACT.Sin)
@@ -198,13 +206,17 @@ def tile_postfiltered_beam_combining_f2_kernel(
         def cross(j):
             t = j % T
             ab[j] = work.tile([P, width(j)], F32, name="ab")
-            nc.scalar.activation(out=ab[j][:], in_=y[j][1], func=ACT.Copy, scale=k_i[:, t : t + 1])
+            if j < A_ON_V:
+                nc.vector.tensor_scalar(out=ab[j][:], in0=y[j][1], scalar1=k_i[:, t : t + 1], scalar2=None, op0=MUL)
+            else:
+                nc.scalar.activation(out=ab[j][:], in_=y[j][1], func=ACT.Copy, scale=k_i[:, t : t + 1])
 
         def power(j):
             w = width(j)
-            if w == 512 and G_COLS:
+            if w >= G_MIN and G_COLS[j // T]:
                 pw[j] = gated.tile([P, w], F32, name="pwg")
-                parts = ((nc.gpsimd, 0, G_COLS), (nc.vector, G_COLS, w))
+                gc = G_COLS[j // T]
+                parts = ((nc.gpsimd, 0, gc),) + (((nc.vector, gc, w),) if gc < w else ())
             else:
                 pw[j] = work.tile([P, w], F32, name="pw")
                 parts = ((nc.vector, 0, w),)
@@ -231,7 +243,10 @@ def tile_postfiltered_beam_combining_f2_kernel(
 
         def inverse(j):
             r2[j] = work.tile([P, width(j)], F32, name="r2")
-            nc.scalar.activation(out=r2[j][:], in_=rs[j][:], func=ACT.Square)
+            if j in R2_ON_V:
+                nc.vector.tensor_tensor(out=r2[j][:], in0=rs[j][:], in1=rs[j][:], op=MUL)
+            else:
+                nc.scalar.activation(out=r2[j][:], in_=rs[j][:], func=ACT.Square)
 
         def wiener(j):
             c, t = divmod(j, T)
@@ -286,22 +301,22 @@ def tile_postfiltered_beam_combining_f2_kernel(
                 nc.vector.tensor_copy(out=res[:], in_=oo[c, b, k][:])
             nc.sync.dma_start(out=out[r0 : r0 + P, :], in_=res[:])
 
-        permute_codes(0, 0, 1)
-        permute_scales(0)
-        permute_codes(0, 1, 3)
-        nc.vector.tensor_scalar(out=den[:, 1:3, :], in0=gn[:], scalar1=TINY, scalar2=None, op0=ADD)
+        permute_codes(0, 0, 2)
         permute_codes(1, 0, 2)
-        nc.vector.reciprocal(out=inv[:], in_=den[:])
-        nc.vector.tensor_copy(out=nz[:], in_=nz_b[:])
+        permute_codes(0, 2, 2)
+        permute_scales(0)
+        nc.vector.tensor_scalar(out=den[:, 1:3, :], in0=gn[:], scalar1=TINY, scalar2=None, op0=ADD)
         permute_codes(1, 2, 2)
+        nc.vector.reciprocal(out=inv[:], in_=den[:])
+        permute_scales(1)
         nc.vector.tensor_tensor(out=rat[:], in0=den[:, 1, :], in1=inv[:, 2, :], op=MUL)
         nc.vector.tensor_tensor(out=kap[:], in0=den[:, 2, :], in1=inv[:, 0, :], op=MUL)
         nc.vector.tensor_tensor(out=dg[:], in0=sd[:], in1=inv[:, 1, :], op=MUL)
+        nc.vector.tensor_copy(out=nz[:], in_=nz_b[:])
         nc.vector.tensor_tensor(out=ratc[:], in0=rat[:], in1=den[:, 0, :], op=MUL)
-        permute_scales(1)
+        nc.vector.tensor_tensor(out=k_u[:], in0=kap[:], in1=dg[:], op=MUL)
         nc.vector.scalar_tensor_tensor(out=k_i[:], in0=ratc[:], scalar=-1.0, in1=sd[:], op0=MUL, op1=MUL)
         nc.vector.tensor_tensor(out=k_r[:], in0=ratc[:], in1=den[:, 0, :], op=MUL)
-        nc.vector.tensor_tensor(out=k_u[:], in0=kap[:], in1=dg[:], op=MUL)
         for j in range(AHEAD):
             steer(j)
         fq = []
@@ -321,9 +336,9 @@ def tile_postfiltered_beam_combining_f2_kernel(
                 square(j)
             if 0 <= j - ARS_LAG < PAIRS:
                 inverse_root(j - ARS_LAG)
-            if j < PAIRS:
+            if A_ON_V <= j < PAIRS:
                 cross(j)
-            if 0 <= j - ARS_LAG < PAIRS:
+            if 0 <= j - ARS_LAG < PAIRS and j - ARS_LAG not in R2_ON_V:
                 inverse(j - ARS_LAG)
             if 0 <= j - WIEN_LAG < PAIRS:
                 wiener(j - WIEN_LAG)
@@ -357,8 +372,12 @@ def tile_postfiltered_beam_combining_f2_kernel(
             while qq and (qq[0][0] < j):
                 quantise_one()
             weigh_some(nf if tail else min(nf, F_FIRST))
+            if j - R2_LAG in R2_ON_V:
+                inverse(j - R2_LAG)
             if 0 <= j - P_LAG < PAIRS:
                 power(j - P_LAG)
+            if j < A_ON_V:
+                cross(j)
             if j + 2 < T:
                 permute_codes(j + 2, 0, 4)
                 permute_scales(j + 2)

from contextlib import ExitStack

import math

import concourse.mybir as mybir

FLOPS = 2 * 1536 * 2048 * 1024 + 2 * 1536 * 1024 * 512

F32 = mybir.dt.float32
BF16 = mybir.dt.bfloat16
I32 = mybir.dt.int32
U32 = mybir.dt.uint32
U8 = mybir.dt.uint8
FP8X4 = mybir.dt.float8_e4m3fn_x4
FP4X4 = mybir.dt.float4_e2m1fn_x4
ACT = mybir.ActivationFunctionType
MUL = mybir.AluOpType.mult
ADD = mybir.AluOpType.add

P = 128
G = 4
T = 4
M = 1536
WIDTHS = [512,512,512]
O_ON_S = [0, 1, 2, 3, 4, 5, 6, 7, 8, 9, 10, 11]
G_COLS = [384, 384, 384]
P_LAG = 1
G_MIN = 512
A_ON_V = 0
R2_ON_V = [0,1,2,3]
R2_LAG = 2
ROT1_LAG = 2
ARS_LAG = 2
ROT_LAG = 1
WIEN_LAG = 3
C_LAG = 1
O_LAG = 0
AHEAD = 1
FI = 4
FB = 256
FB_LAST = 128
BUFS = 5
TINY = 1.3e-18
O_BUFS = 2
F_FIRST = 1


def tile_postfiltered_beam_combining_f2_kernel(
    tc, x_words, x_scales, s_words, s_scales, phi, noise, gain, c_words, c_scales, out
):
    nc = tc.nc
    CH = len(WIDTHS)
    PAIRS = CH * T
    START = [sum(WIDTHS[:c]) for c in range(CH)]
    W0 = WIDTHS[0]
    with ExitStack() as ctx:
        keep = ctx.enter_context(tc.tile_pool(name="keep", bufs=1))
        work = ctx.enter_context(tc.tile_pool(name="work", bufs=BUFS))
        gated = ctx.enter_context(tc.tile_pool(name="gated", bufs=2))
        wide = ctx.enter_context(tc.tile_pool(name="wide", bufs=3))
        psum = ctx.enter_context(tc.psum_pool(name="psum", bufs=8 - O_BUFS))
        psum_o = ctx.enter_context(tc.psum_pool(name="psum_o", bufs=O_BUFS))
        ctx.enter_context(tc.manual_schedule())

        s_raw = keep.tile([P, G, 2048], U8, align_bytes=64)
        s_sraw = keep.tile([P, G, 1024], U8, align_bytes=64)
        s_cod = [keep.tile([P, G, 2, 256], U8, name="s_cod%d" % t, align_bytes=64) for t in range(T)]
        s_sca = [keep.tile([P, G, 2, 128], U8, name="s_sca%d" % t, align_bytes=64) for t in range(T)]
        x_cod = [keep.tile([P, G, 2 * w], U8, name="x_cod%d" % c, align_bytes=64) for c, w in enumerate(WIDTHS)]
        x_sca0 = keep.tile([P, G, W0], U8, align_bytes=64)
        x_scar = keep.tile([P, G, M - W0], U8, align_bytes=64)
        c_cod = keep.tile([P, 2, 1024], U8, align_bytes=64)
        c_sca = keep.tile([P, 2, 512], U8, align_bytes=64)
        ph = keep.tile([P, T], BF16)
        nz_b = keep.tile([P, T], BF16)
        gn = keep.tile([P, 2, T], BF16)
        nz = keep.tile([P, T], F32)
        sd = keep.tile([P, T], F32)
        sh = keep.tile([P, T], F32)
        shsq = keep.tile([P, T], F32)
        den = keep.tile([P, 3, T], F32)
        inv = keep.tile([P, 3, T], F32)
        rat = keep.tile([P, T], F32)
        ratc = keep.tile([P, T], F32)
        dg = keep.tile([P, T], F32)
        k_r = keep.tile([P, T], F32)
        k_i = keep.tile([P, T], F32)
        k_u = keep.tile([P, T], F32)
        kap = keep.tile([P, T], F32)
        warm = keep.tile([P, T], F32)
        warm1 = keep.tile([P, T], F32)
        warm2 = keep.tile([P, T], F32)

        def fill_zero(eng, plane):
            eng.memset(plane[:].rearrange("p g n -> p (g n)").bitcast(I32), 0)

        xs_view = x_scales.rearrange("g (q r) n -> q r g n", r=4)
        ss_view = s_scales.rearrange("g (q r) n -> q r g n", r=4)
        cs_view = c_scales.rearrange("g (q r) n -> q r g n", r=4)
        xw_view = x_words.rearrange("g p b -> p g b")
        cw_view = c_words.rearrange("g p b -> p g b")

        def load_x(c):
            a = 2 * START[c]
            nc.sync.dma_start(out=x_cod[c][:].bitcast(I32), in_=xw_view[:, :, a : a + 2 * WIDTHS[c]].bitcast(I32))

        def load_rows(eng, plane, view, quarters=range(4)):
            for q in quarters:
                eng.dma_start(out=plane[32 * q : 32 * q + 4, :, :].bitcast(I32), in_=view[q].bitcast(I32))

        nc.vector.memset(warm[:], 0.0)
        fill_zero(nc.vector, s_sraw)
        fill_zero(nc.vector, x_sca0)
        nc.gpsimd.dma_start(out=ph[:], in_=phi.rearrange("(p t) -> p t", t=T))
        nc.gpsimd.dma_start(out=gn[:], in_=gain.rearrange("(h p t) -> p h t", h=2, t=T))
        nc.gpsimd.dma_start(out=nz_b[:], in_=noise.rearrange("(p t) -> p t", t=T))
        load_rows(nc.scalar, s_sraw, ss_view)
        nc.scalar.activation(out=warm1[:], in_=warm[:], func=ACT.Sin)
        sw_view = s_words.rearrange("g p b -> p g b")
        def load_s(g):
            nc.sync.dma_start(out=s_raw[:, g : g + 2, :].bitcast(I32), in_=sw_view[:, g : g + 2, :].bitcast(I32))

        load_s(0)
        load_rows(nc.sync, x_sca0, xs_view[:, :, :, 0:W0], (0,))
        load_s(2)
        load_x(0)
        load_rows(nc.sync, x_sca0, xs_view[:, :, :, 0:W0], (1, 2, 3))
        load_x(1)

        nc.scalar.activation(out=sd[:], in_=ph[:], func=ACT.Sin)
        nc.scalar.activation(out=sh[:], in_=ph[:], func=ACT.Sin, scale=0.5)
        nc.scalar.activation(out=shsq[:], in_=sh[:], func=ACT.Square, scale=math.sqrt(2.0))
        nc.scalar.activation(out=den[:, 0, :], in_=shsq[:], func=ACT.Copy, scale=-1.0, bias=1.0)
        nc.scalar.activation(out=warm2[:], in_=warm[:], func=ACT.Abs_reciprocal_sqrt, bias=1.0)
        fill_zero(nc.gpsimd, x_scar)
        fill_zero(nc.gpsimd, c_sca)

        load_rows(nc.sync, x_scar, xs_view[:, :, :, W0:M])
        for c in range(2, CH):
            load_x(c)
        load_rows(nc.sync, c_sca, cs_view)
        nc.sync.dma_start(out=c_cod[:].bitcast(I32), in_=cw_view.bitcast(I32))

        def permute_codes(t, g, n):
            nc.vector.tensor_copy(
                out=s_cod[t][:, g : g + n, :, :].rearrange("p g h (m e) -> p (g h) m e", e=2),
                in_=s_raw[:, g : g + n, :].rearrange("p g (h m t e) -> p (g h) m t e", h=2, t=T, e=2)[:, :, :, t, :],
            )

        def permute_scales(t):
            nc.vector.tensor_copy(
                out=s_sca[t][:].rearrange("p g h m -> p (g h) m"),
                in_=s_sraw[:].rearrange("p g (h m t) -> p (g h) m t", h=2, t=T)[:, :, :, t],
            )

        y = {}
        sq = {}
        ab = {}
        pw = {}
        rs = {}
        r2 = {}
        uv = {}
        ff = {}
        zt = {}
        zc = {}
        zs = {}
        oo = {}

        def fb(c):
            return min(FB if c < CH - 1 else FB_LAST, WIDTHS[c])

        def width(j):
            return WIDTHS[j // T]

        def steer(j):
            c, t = divmod(j, T)
            w = WIDTHS[c]
            if w == 512:
                yr = psum.tile([P, 512], F32, name="y")
                yi = psum.tile([P, 512], F32, name="y")
                y[j] = (yr[:], yi[:])
            else:
                yy = psum.tile([P, 2, w], F32, name="y")
                y[j] = (yy[:, 0, :], yy[:, 1, :], yy[:])
            for h in range(2):
                for g in range(G):
                    nc.tensor.matmul_mx(
                        out=y[j][h],
                        lhsT=s_cod[t][:, g, h, :].bitcast(FP4X4),
                        lhsT_scale=s_sca[t][:, g, h, :],
                        rhs=x_cod[c][:, g, :].bitcast(FP4X4),
                        rhs_scale=x_sca0[:, g, :] if c == 0 else x_scar[:, g, START[c] - W0 : START[c] - W0 + w],
                        start=(g == 0),
                        stop=(g == G - 1),
                    )

        def square(j):
            w = width(j)
            sq[j] = work.tile([P, 2, w], F32, name="sq")
            if w == 512:
                for h in range(2):
                    nc.scalar.activation(out=sq[j][:, h, :], in_=y[j][h], func=ACT.Square)
            else:
                nc.scalar.activation(out=sq[j][:], in_=y[j][2], func=ACT.Square)

        def cross(j):
            t = j % T
            ab[j] = work.tile([P, width(j)], F32, name="ab")
            if j < A_ON_V:
                nc.vector.tensor_scalar(out=ab[j][:], in0=y[j][1], scalar1=k_i[:, t : t + 1], scalar2=None, op0=MUL)
            else:
                nc.scalar.activation(out=ab[j][:], in_=y[j][1], func=ACT.Copy, scale=k_i[:, t : t + 1])

        def power(j):
            w = width(j)
            if w >= G_MIN and G_COLS[j // T]:
                pw[j] = gated.tile([P, w], F32, name="pwg")
                gc = G_COLS[j // T]
                parts = ((nc.gpsimd, 0, gc),) + (((nc.vector, gc, w),) if gc < w else ())
            else:
                pw[j] = work.tile([P, w], F32, name="pw")
                parts = ((nc.vector, 0, w),)
            for eng, a, b in parts:
                eng.tensor_tensor(out=pw[j][:, a:b], in0=sq[j][:, 0, a:b], in1=sq[j][:, 1, a:b], op=ADD)

        def rotate(j, h):
            c, t = divmod(j, T)
            if t == 0 and h == 0:
                uv[c] = wide.tile([P, T, 2, width(j)], F32, name="uv")
            if h == 0:
                nc.vector.scalar_tensor_tensor(
                    out=uv[c][:, t, 0, :], in0=y[j][0], scalar=k_r[:, t : t + 1], in1=ab[j][:], op0=MUL, op1=ADD
                )
            else:
                nc.vector.scalar_tensor_tensor(
                    out=uv[c][:, t, 1, :], in0=uv[c][:, t, 0, :], scalar=k_u[:, t : t + 1], in1=y[j][1], op0=MUL, op1=ADD
                )

        def inverse_root(j):
            t = j % T
            rs[j] = work.tile([P, width(j)], F32, name="rs")
            nc.scalar.activation(out=rs[j][:], in_=pw[j][:], func=ACT.Abs_reciprocal_sqrt, bias=nz[:, t : t + 1])

        def inverse(j):
            r2[j] = work.tile([P, width(j)], F32, name="r2")
            if j in R2_ON_V:
                nc.vector.tensor_tensor(out=r2[j][:], in0=rs[j][:], in1=rs[j][:], op=MUL)
            else:
                nc.scalar.activation(out=r2[j][:], in_=rs[j][:], func=ACT.Square)

        def wiener(j):
            c, t = divmod(j, T)
            if t == 0:
                ff[c] = wide.tile([P, T, width(j)], F32, name="ff")
            nc.vector.scalar_tensor_tensor(
                out=ff[c][:, t, :], in0=pw[j][:], scalar=kap[:, t : t + 1], in1=r2[j][:], op0=MUL, op1=MUL
            )

        def weigh(c, b, h):
            n = fb(c)
            if h == 0:
                zt[c, b] = work.tile([P, 2, n, T], BF16, name="zt", align_bytes=64)
            cols = slice(b * n, (b + 1) * n)
            nc.vector.tensor_tensor(
                out=zt[c, b][:, h, :, :].rearrange("p (c i) t -> p c t i", i=FI),
                in0=uv[c][:, :, h, cols].rearrange("p t (c i) -> p c t i", i=FI),
                in1=ff[c][:, :, cols].rearrange("p t (c i) -> p c t i", i=FI),
                op=MUL,
            )

        def quantise(c, b):
            n = fb(c)
            zc[c, b] = work.tile([P, 2, n], U32, name="zc", align_bytes=64)
            zs[c, b] = work.tile([P, 2, n], U8, name="zs", align_bytes=64)
            nc.vector.quantize_mx(
                out=zc[c, b][:].rearrange("p h n -> p (h n)").bitcast(FP8X4),
                scales=zs[c, b][:].rearrange("p h n -> p (h n)"),
                in_=zt[c, b][:].rearrange("p h n t -> p (h n t)"),
            )

        def combine(c, b, k):
            o = psum_o.tile([P, 512], F32, name="o")
            oo[c, b, k] = o
            for h in range(2):
                nc.tensor.matmul_mx(
                    out=o[:],
                    lhsT=zc[c, b][:, h, k * P : (k + 1) * P].bitcast(FP8X4),
                    lhsT_scale=zs[c, b][:, h, k * P : (k + 1) * P],
                    rhs=c_cod[:, h, :].bitcast(FP4X4),
                    rhs_scale=c_sca[:, h, :],
                    start=(h == 0),
                    stop=(h == 1),
                )

        def store(c, b, k):
            r0 = START[c] + b * fb(c) + k * P
            res = work.tile([P, 512], F32, name="res")
            if r0 // P in O_ON_S:
                nc.scalar.copy(out=res[:], in_=oo[c, b, k][:])
            else:
                nc.vector.tensor_copy(out=res[:], in_=oo[c, b, k][:])
            nc.sync.dma_start(out=out[r0 : r0 + P, :], in_=res[:])

        permute_codes(0, 0, 2)
        permute_codes(1, 0, 2)
        permute_codes(0, 2, 2)
        permute_scales(0)
        nc.vector.tensor_scalar(out=den[:, 1:3, :], in0=gn[:], scalar1=TINY, scalar2=None, op0=ADD)
        permute_codes(1, 2, 2)
        nc.vector.reciprocal(out=inv[:], in_=den[:])
        permute_scales(1)
        nc.vector.tensor_tensor(out=rat[:], in0=den[:, 1, :], in1=inv[:, 2, :], op=MUL)
        nc.vector.tensor_tensor(out=kap[:], in0=den[:, 2, :], in1=inv[:, 0, :], op=MUL)
        nc.vector.tensor_tensor(out=dg[:], in0=sd[:], in1=inv[:, 1, :], op=MUL)
        nc.vector.tensor_copy(out=nz[:], in_=nz_b[:])
        nc.vector.tensor_tensor(out=ratc[:], in0=rat[:], in1=den[:, 0, :], op=MUL)
        nc.vector.tensor_tensor(out=k_u[:], in0=kap[:], in1=dg[:], op=MUL)
        nc.vector.scalar_tensor_tensor(out=k_i[:], in0=ratc[:], scalar=-1.0, in1=sd[:], op0=MUL, op1=MUL)
        nc.vector.tensor_tensor(out=k_r[:], in0=ratc[:], in1=den[:, 0, :], op=MUL)
        for j in range(AHEAD):
            steer(j)
        fq = []
        qq = []
        cq = []
        oq = []
        nf = 0
        for j in range(PAIRS + 20):
            tail = j >= PAIRS
            while cq and cq[0][0] <= j:
                k = cq.pop(0)[1:]
                while len(oq) >= O_BUFS:
                    store(*oq.pop(0)[1:])
                combine(*k)
                oq.append((j + O_LAG,) + k)
            if j < PAIRS:
                square(j)
            if 0 <= j - ARS_LAG < PAIRS:
                inverse_root(j - ARS_LAG)
            if A_ON_V <= j < PAIRS:
                cross(j)
            if 0 <= j - ARS_LAG < PAIRS and j - ARS_LAG not in R2_ON_V:
                inverse(j - ARS_LAG)
            if 0 <= j - WIEN_LAG < PAIRS:
                wiener(j - WIEN_LAG)
                if (j - WIEN_LAG) % T == T - 1:
                    c = (j - WIEN_LAG) // T
                    n = fb(c)
                    nf = -(-2 * (WIDTHS[c] // n) // T)
                    for b in range(WIDTHS[c] // n):
                        fq += [(c, b, 0), (c, b, 1)]
            if 0 <= j - ROT_LAG < PAIRS:
                rotate(j - ROT_LAG, 0)
            if 0 <= j - ROT1_LAG < PAIRS:
                rotate(j - ROT1_LAG, 1)

            def weigh_some(n):
                for i in range(n):
                    if fq:
                        c, b, h = fq.pop(0)
                        weigh(c, b, h)
                        if h == 1:
                            qq.append((j - (1 if tail else 0), c, b))
                        if tail and qq and h == 0:
                            quantise_one()

            def quantise_one():
                c, b = qq.pop(0)[1:]
                quantise(c, b)
                for k in range(fb(c) // P):
                    cq.append((j + (0 if tail else C_LAG), c, b, k))

            while qq and (qq[0][0] < j):
                quantise_one()
            weigh_some(nf if tail else min(nf, F_FIRST))
            if j - R2_LAG in R2_ON_V:
                inverse(j - R2_LAG)
            if 0 <= j - P_LAG < PAIRS:
                power(j - P_LAG)
            if j < A_ON_V:
                cross(j)
            if j + 2 < T:
                permute_codes(j + 2, 0, 4)
                permute_scales(j + 2)
            weigh_some(2 if tail else nf - min(nf, F_FIRST))
            if j + AHEAD < PAIRS:
                steer(j + AHEAD)
            while oq and oq[0][0] <= j:
                store(*oq.pop(0)[1:])
